import numpy as np, ml_dtypes
CORES = [0,1,16,17,32,33,48,49,64,65,80,81,96,97,112,113]
N = 16
G1 = [0,1,2,3,4,5,6,7,8,9,10,11,12,13,14,15]
ROOT1 = 3
G2 = [8,9,10,11,12,13,14,15]
def setup_inputs(rng):
    return {"x1": rng.standard_normal((N, 128, 1024), dtype=np.float32).astype(ml_dtypes.bfloat16), "x2": rng.standard_normal((N, 128, 8), dtype=np.float32)}
def reference(x1, x2):
    out = {}
    y = np.full((N, 128, 1024), np.nan, x1.dtype)
    for r in G1:
        y[r] = x1[G1[ROOT1]]
    out["y1"] = y
    y = np.full((N, 128, 8), np.nan, x2.dtype)
    s = x2[G2].max(axis=0)
    for r in G2:
        y[r] = s
    out["y2"] = y
    return out

@@ -1,0 +1,230 @@
+from concourse.bass import DstId, RemoteDMATransfer
+
+ROWS, COLS = 128, 1024
+N_EARLY, W_EARLY = 8, 76
+N_LATE, W_LATE = 8, 52
+R_EARLY = N_EARLY * 128 * W_EARLY // COLS
+N2, W2 = 8, 8
+
+SCRATCH = {
+    "landE": ("dram", [N_EARLY, 128, W_EARLY], "bfloat16"),
+    "landL": ("dram", [N_LATE, 128, W_LATE], "bfloat16"),
+    "holdE": ("dram", [128, W_EARLY], "bfloat16"),
+    "holdL": ("dram", [128, W_LATE], "bfloat16"),
+    "x2s": ("dram", [128, W2], "float32"),
+    "gat": ("dram", [N2, 128, W2], "float32"),
+    "res": ("dram", [128, W2], "float32"),
+}
+SEMAPHORES = ["ldE", "ldL", "go", "left", "got", "arrE", "arrL", "stE", "stL", "stY",
+              "ld2", "left2", "gat2", "arr2", "st2"]
+
+
+def _bits(mask):
+    return [b for b in range(mask.bit_length()) if (mask >> b) & 1]
+
+
+def _mask(bits):
+    m = 0
+    for b in bits:
+        m |= 1 << b
+    return m
+
+
+def _common(topo, src, dests):
+    m = topo.mask(src, dests[0])
+    for d in dests:
+        m &= topo.mask(src, d)
+    return _bits(m)
+
+
+def _lanes(topo, src, dests):
+    far = [d for d in dests if topo.chip(d) != topo.chip(src)]
+    near = [d for d in dests if topo.chip(d) == topo.chip(src)]
+    fb = _common(topo, src, far) if far else []
+    nb = [b for b in _common(topo, src, near) if b not in fb] if near else []
+    return far, fb, near, nb
+
+
+def _fan(topo, src, dests):
+    far, fb, near, nb = _lanes(topo, src, dests)
+    out = []
+    for grp, bits in ((far, fb), (near, nb)):
+        if not grp:
+            continue
+        t = len(bits)
+        while len(grp) % t:
+            t //= 2
+        per, n = len(bits) // t, len(grp) // t
+        for j in range(t):
+            out.append((grp[j * n:(j + 1) * n], bits[j * per:(j + 1) * per]))
+    return out
+
+
+def _layout(T, topo):
+    tab = T.tables
+    mem1 = [T.cores[r] for r in tab["G1"]]
+    root = mem1[tab["ROOT1"]]
+    mem2 = [T.cores[r] for r in tab["G2"]]
+    every = range(topo.CHIPS * topo.CORES_PER_CHIP)
+    group = set(T.cores)
+    home = topo.chip(root)
+    ring = []
+    for c in mem1:
+        if topo.chip(c) not in ring:
+            ring.append(topo.chip(c))
+    k = ring.index(home)
+    ring = ring[k:] + ring[:k]
+    far_ranks = [c for c in mem1 if topo.chip(c) != home]
+
+    def spare(ch):
+        return [c for c in every if topo.chip(c) == ch and c not in group]
+
+    def reaches(c):
+        return all(topo.may_write(c, t) for t in far_ranks if t != c)
+
+    away = []
+    for ch in ring[1:]:
+        dies = []
+        for c in spare(ch):
+            if topo.die(c) not in dies and reaches(c) and topo.may_write(root, c):
+                dies.append(topo.die(c))
+                away.append(c)
+    local = [c for c in spare(home) if topo.die(c) != topo.die(root) and reaches(c)]
+    local = local[:N_EARLY + N_LATE - len(away)]
+    early, late = away[:N_EARLY], away[N_EARLY:] + local
+    assert len(early) == N_EARLY and len(late) == N_LATE
+
+    def targets(h):
+        i = ring.index(topo.chip(h))
+        order = ring[i:] + ring[:i]
+        return [c for ch in order if ch != home for c in mem1 if topo.chip(c) == ch]
+
+    folders = []
+    for m in mem2:
+        ch = topo.chip(m)
+        if any(topo.chip(f) == ch for f in folders):
+            continue
+        free = [c for c in spare(ch) if c not in away and c not in local
+                and all(topo.may_write(x, c) for x in mem2)]
+        same = [c for c in free if topo.die(c) == topo.die(m)]
+        folders.append((same or free)[0])
+    return dict(mem1=mem1, root=root, mem2=mem2, home=home, early=early, late=late, local=local,
+                targets=targets, folders=folders,
+                near_ranks=[c for c in mem1 if topo.chip(c) == home and c != root])
+
+
+def _ids(topo, dests):
+    out = []
+    for d in dests:
+        rid, pid, _ = topo.addr(d)
+        out.append(DstId(rid=rid, pnc=pid))
+    return out
+
+
+def _xfer(topo, dests, bits, sem, srcs, dst_ap, alu_op=0):
+    return RemoteDMATransfer(dst_ids=_ids(topo, dests), dma_engine_mask=_mask(bits), remote_sem=sem,
+                             srcs=srcs, dsts=[dst_ap for _ in dests], alu_op=alu_op)
+
+
+def rank_program(g, core, T, topo):
+    L = _layout(T, topo)
+    root, early, late, local = L["root"], L["early"], L["late"], L["local"]
+    sem = T.sem
+
+    if core in L["mem2"]:
+        g.sync.dma_start(T.x2s[:], T.x2[:]).then_inc(sem.ld2, 16)
+
+    if core == root:
+        g.sync.dma_start(T.landE[:], T.x1[0:R_EARLY, :]).then_inc(sem.ldE, 16)
+        g.scalar.dma_start(T.landL[:], T.x1[R_EARLY:ROWS, :]).then_inc(sem.ldL, 16)
+        g.scalar.wait_ge(sem.go, 1)
+        g.scalar.dma_start(T.y1[:], T.x1[:]).then_inc(sem.stY, 16)
+        g.scalar.wait_ge(sem.stY, 16)
+    elif core in L["mem1"]:
+        n_e = n_l = 0
+        if core in L["near_ranks"]:
+            n_e, n_l = N_EARLY, N_LATE
+        else:
+            for h in early + late:
+                for dests, bits in _fan(topo, h, L["targets"](h)):
+                    if core in dests:
+                        if h in early:
+                            n_e += len(bits)
+                        else:
+                            n_l += len(bits)
+        g.sync.wait_ge(sem.arrE, n_e)
+        g.sync.dma_start(T.y1[0:R_EARLY, :], T.landE[:]).then_inc(sem.stE, 16)
+        g.sync.wait_ge(sem.stE, 16)
+        g.scalar.wait_ge(sem.arrL, n_l)
+        g.scalar.dma_start(T.y1[R_EARLY:ROWS, :], T.landL[:]).then_inc(sem.stL, 16)
+        g.scalar.wait_ge(sem.stL, 16)
+
+    if core == root:
+        _, fb, _, nb = _lanes(topo, root, early + late)
+        left = 0
+        g.wait_ge(sem.ldE, 16)
+        call = [_xfer(topo, [h], [fb[i]], sem.got, [T.landE[i]], T.holdE[:]) for i, h in enumerate(early)]
+        g.remote_dma_fused(call, local_sem=sem.left)
+        left += len(call)
+        g.wait_ge(sem.ldL, 16)
+        call = []
+        per = len(nb) // len(local)
+        for i, h in enumerate(late):
+            if h in local:
+                j = local.index(h)
+                bits = nb[j * per:(j + 1) * per]
+            else:
+                bits = [fb[i]]
+            call.append(_xfer(topo, [h], bits, sem.got, [T.landL[i]], T.holdL[:]))
+            left += len(bits)
+        g.remote_dma_fused(call, local_sem=sem.left)
+        g.sem_inc(sem.go, 1)
+        near = L["near_ranks"]
+        if near:
+            call = [_xfer(topo, near, [nb[i]], sem.arrE, [T.landE[i]], T.landE[i]) for i in range(N_EARLY)]
+            g.remote_dma_fused(call, local_sem=sem.left)
+            left += len(call)
+            call = [_xfer(topo, near, [nb[i]], sem.arrL, [T.landL[i]], T.landL[i]) for i in range(N_LATE)]
+            g.remote_dma_fused(call, local_sem=sem.left)
+            left += len(call)
+        g.wait_ge(sem.left, left)
+
+    if core in early or core in late:
+        if core in early:
+            i, hold, land, arr, got = early.index(core), T.holdE, T.landE, sem.arrE, 1
+        else:
+            i, hold, land, arr = late.index(core), T.holdL, T.landL, sem.arrL
+            _, _, _, nb = _lanes(topo, root, early + late)
+            got = len(nb) // len(local) if core in local else 1
+        fan = _fan(topo, core, L["targets"](core))
+        g.wait_ge(sem.got, got)
+        g.remote_dma_fused([_xfer(topo, dests, bits, arr, [hold[:]], land[i]) for dests, bits in fan],
+                           local_sem=sem.left)
+        g.wait_ge(sem.left, sum(len(bits) for _, bits in fan))
+
+    mem2, folders = L["mem2"], L["folders"]
+    if core in mem2:
+        m = mem2.index(core)
+        fan = _fan(topo, core, folders)
+        g.wait_ge(sem.ld2, 16)
+        g.remote_dma_fused([_xfer(topo, dests, bits, sem.gat2, [T.x2s[:]], T.gat[m]) for dests, bits in fan],
+                           local_sem=sem.left2)
+        mine = [f for f in folders if topo.chip(f) == topo.chip(core)][0]
+        kin = [c for c in mem2 if topo.chip(c) == topo.chip(core)]
+        n = sum(len(bits) for dests, bits in _fan(topo, mine, kin) if core in dests)
+        g.wait_ge(sem.arr2, n)
+        g.dma_start(T.y2[:], T.res[:]).then_inc(sem.st2, 16)
+        g.wait_ge(sem.st2, 16)
+        g.wait_ge(sem.left2, sum(len(bits) for _, bits in fan))
+
+    if core in folders:
+        n = 0
+        for c in mem2:
+            n += sum(len(bits) for dests, bits in _fan(topo, c, folders) if core in dests)
+        kin = [c for c in mem2 if topo.chip(c) == topo.chip(core)]
+        fan = _fan(topo, core, kin)
+        slots = [T.gat[m] for m in range(len(mem2))]
+        g.wait_ge(sem.gat2, n)
+        g.remote_dma_fused([_xfer(topo, dests, bits, sem.arr2, slots, T.res[:], alu_op=2) for dests, bits in fan],
+                           local_sem=sem.left2)
+        g.wait_ge(sem.left2, sum(len(bits) for _, bits in fan))

@@ -1,22 +1,27 @@
 from concourse.bass import DstId, RemoteDMATransfer
 
 ROWS, COLS = 128, 1024
-N_EARLY, W_EARLY = 8, 76
-N_LATE, W_LATE = 8, 52
-R_EARLY = N_EARLY * 128 * W_EARLY // COLS
+W = {"A": 48, "B": 52, "C": 29}
+NP = {"A": 10, "B": 6, "C": 8}
+ROW0 = {"A": 0, "B": 60, "C": 99}
+N_FIRST = 8
+GROUPS = (("A", "A", 0, 8), ("X", "A", 8, 10), ("B", "B", 0, 6), ("C", "C", 0, 8))
 N2, W2 = 8, 8
 
 SCRATCH = {
-    "landE": ("dram", [N_EARLY, 128, W_EARLY], "bfloat16"),
-    "landL": ("dram", [N_LATE, 128, W_LATE], "bfloat16"),
-    "holdE": ("dram", [128, W_EARLY], "bfloat16"),
-    "holdL": ("dram", [128, W_LATE], "bfloat16"),
+    "landA": ("dram", [NP["A"], 128, W["A"]], "bfloat16"),
+    "landB": ("dram", [NP["B"], 128, W["B"]], "bfloat16"),
+    "landC": ("dram", [NP["C"], 128, W["C"]], "bfloat16"),
+    "holdA": ("dram", [128, W["A"]], "bfloat16"),
+    "holdB": ("dram", [128, W["B"]], "bfloat16"),
+    "holdC": ("dram", [128, W["C"]], "bfloat16"),
+    "full": ("dram", [ROWS, COLS], "bfloat16"),
     "x2s": ("dram", [128, W2], "float32"),
     "gat": ("dram", [N2, 128, W2], "float32"),
     "res": ("dram", [128, W2], "float32"),
 }
-SEMAPHORES = ["ldE", "ldL", "go", "left", "got", "arrE", "arrL", "stE", "stL", "stY",
-              "ld2", "left2", "gat2", "arr2", "st2"]
+SEMAPHORES = ["ldA", "ldB", "ldC", "ldF", "go", "left", "gA", "gB", "gC", "aA", "aX", "aB", "aC", "aF",
+              "stS", "stC", "ld2", "left2", "gat2", "arr2", "st2"]
 
 
 def _bits(mask):
@@ -60,6 +65,10 @@ def _fan(topo, src, dests):
     return out
 
 
+def _group(kind, slot):
+    return [gr[0] for gr in GROUPS if gr[1] == kind and gr[2] <= slot < gr[3]][0]
+
+
 def _layout(T, topo):
     tab = T.tables
     mem1 = [T.cores[r] for r in tab["G1"]]
@@ -89,15 +98,15 @@ def _layout(T, topo):
             if topo.die(c) not in dies and reaches(c) and topo.may_write(root, c):
                 dies.append(topo.die(c))
                 away.append(c)
-    local = [c for c in spare(home) if topo.die(c) != topo.die(root) and reaches(c)]
-    local = local[:N_EARLY + N_LATE - len(away)]
-    early, late = away[:N_EARLY], away[N_EARLY:] + local
-    assert len(early) == N_EARLY and len(late) == N_LATE
+    local = [c for c in spare(home) if topo.die(c) != topo.die(root) and reaches(c)][:NP["A"] - N_FIRST]
+    holders = {"A": away[:N_FIRST] + local, "B": away[N_FIRST:], "C": away[:N_FIRST]}
+    for kind in NP:
+        assert len(holders[kind]) == NP[kind]
 
-    def targets(h):
+    def fan(h):
         i = ring.index(topo.chip(h))
         order = ring[i:] + ring[:i]
-        return [c for ch in order if ch != home for c in mem1 if topo.chip(c) == ch]
+        return _fan(topo, h, [c for ch in order if ch != home for c in mem1 if topo.chip(c) == ch])
 
     folders = []
     for m in mem2:
@@ -108,8 +117,7 @@ def _layout(T, topo):
                 and all(topo.may_write(x, c) for x in mem2)]
         same = [c for c in free if topo.die(c) == topo.die(m)]
         folders.append((same or free)[0])
-    return dict(mem1=mem1, root=root, mem2=mem2, home=home, early=early, late=late, local=local,
-                targets=targets, folders=folders,
+    return dict(mem1=mem1, root=root, mem2=mem2, home=home, holders=holders, local=local, fan=fan, folders=folders,
                 near_ranks=[c for c in mem1 if topo.chip(c) == home and c != root])
 
 
@@ -128,81 +136,79 @@ def _xfer(topo, dests, bits, sem, srcs, dst_ap, alu_op=0):
 
 def rank_program(g, core, T, topo):
     L = _layout(T, topo)
-    root, early, late, local = L["root"], L["early"], L["late"], L["local"]
+    root, holders, local = L["root"], L["holders"], L["local"]
+    mem2, folders = L["mem2"], L["folders"]
     sem = T.sem
+    land = {"A": T.landA, "B": T.landB, "C": T.landC}
+    hold = {"A": T.holdA, "B": T.holdB, "C": T.holdC}
 
-    if core in L["mem2"]:
+    def rows(kind, lo, hi):
+        return ROW0[kind] + lo * W[kind] // 8, ROW0[kind] + hi * W[kind] // 8
+
+    if core in mem2:
         g.sync.dma_start(T.x2s[:], T.x2[:]).then_inc(sem.ld2, 16)
 
     if core == root:
-        g.sync.dma_start(T.landE[:], T.x1[0:R_EARLY, :]).then_inc(sem.ldE, 16)
-        g.scalar.dma_start(T.landL[:], T.x1[R_EARLY:ROWS, :]).then_inc(sem.ldL, 16)
+        for kind, q in (("A", g.sync), ("B", g.scalar), ("C", g.sync)):
+            r0, r1 = rows(kind, 0, NP[kind])
+            q.dma_start(land[kind][:], T.x1[r0:r1, :]).then_inc(sem["ld" + kind], 16)
+        if L["near_ranks"]:
+            g.scalar.dma_start(T.full[:], T.x1[:]).then_inc(sem.ldF, 16)
         g.scalar.wait_ge(sem.go, 1)
-        g.scalar.dma_start(T.y1[:], T.x1[:]).then_inc(sem.stY, 16)
-        g.scalar.wait_ge(sem.stY, 16)
+        g.scalar.dma_start(T.y1[:], T.x1[:]).then_inc(sem.stC, 16)
+        g.scalar.wait_ge(sem.stC, 16)
+    elif core in L["near_ranks"]:
+        _, _, _, nb = _lanes(topo, root, holders["A"])
+        g.sync.wait_ge(sem.aF, len(nb))
+        g.sync.dma_start(T.y1[:], T.full[:]).then_inc(sem.stS, 16)
+        g.sync.wait_ge(sem.stS, 16)
     elif core in L["mem1"]:
-        n_e = n_l = 0
-        if core in L["near_ranks"]:
-            n_e, n_l = N_EARLY, N_LATE
-        else:
-            for h in early + late:
-                for dests, bits in _fan(topo, h, L["targets"](h)):
-                    if core in dests:
-                        if h in early:
-                            n_e += len(bits)
-                        else:
-                            n_l += len(bits)
-        g.sync.wait_ge(sem.arrE, n_e)
-        g.sync.dma_start(T.y1[0:R_EARLY, :], T.landE[:]).then_inc(sem.stE, 16)
-        g.sync.wait_ge(sem.stE, 16)
-        g.scalar.wait_ge(sem.arrL, n_l)
-        g.scalar.dma_start(T.y1[R_EARLY:ROWS, :], T.landL[:]).then_inc(sem.stL, 16)
-        g.scalar.wait_ge(sem.stL, 16)
+        for q, st, names in ((g.sync, sem.stS, ("A", "C")), (g.scalar, sem.stC, ("B", "X"))):
+            for name in names:
+                _, kind, lo, hi = [gr for gr in GROUPS if gr[0] == name][0]
+                n = 0
+                for s in range(lo, hi):
+                    n += sum(len(bits) for dests, bits in L["fan"](holders[kind][s]) if core in dests)
+                r0, r1 = rows(kind, lo, hi)
+                q.wait_ge(sem["a" + name], n)
+                q.dma_start(T.y1[r0:r1, :], land[kind][lo:hi]).then_inc(st, 16)
+            q.wait_ge(st, 16 * len(names))
 
+    _, fb, _, nb = _lanes(topo, root, holders["A"])
+    per = len(nb) // len(local)
     if core == root:
-        _, fb, _, nb = _lanes(topo, root, early + late)
         left = 0
-        g.wait_ge(sem.ldE, 16)
-        call = [_xfer(topo, [h], [fb[i]], sem.got, [T.landE[i]], T.holdE[:]) for i, h in enumerate(early)]
-        g.remote_dma_fused(call, local_sem=sem.left)
-        left += len(call)
-        g.wait_ge(sem.ldL, 16)
-        call = []
-        per = len(nb) // len(local)
-        for i, h in enumerate(late):
-            if h in local:
-                j = local.index(h)
-                bits = nb[j * per:(j + 1) * per]
-            else:
-                bits = [fb[i]]
-            call.append(_xfer(topo, [h], bits, sem.got, [T.landL[i]], T.holdL[:]))
-            left += len(bits)
-        g.remote_dma_fused(call, local_sem=sem.left)
+        for kind in ("A", "B", "C"):
+            g.wait_ge(sem["ld" + kind], 16)
+            call = []
+            for i, h in enumerate(holders[kind]):
+                if h in local:
+                    j = local.index(h)
+                    bits = nb[j * per:(j + 1) * per]
+                else:
+                    bits = [fb[i]]
+                call.append(_xfer(topo, [h], bits, sem["g" + kind], [land[kind][i]], hold[kind][:]))
+                left += len(bits)
+            g.remote_dma_fused(call, local_sem=sem.left)
         g.sem_inc(sem.go, 1)
-        near = L["near_ranks"]
-        if near:
-            call = [_xfer(topo, near, [nb[i]], sem.arrE, [T.landE[i]], T.landE[i]) for i in range(N_EARLY)]
-            g.remote_dma_fused(call, local_sem=sem.left)
-            left += len(call)
-            call = [_xfer(topo, near, [nb[i]], sem.arrL, [T.landL[i]], T.landL[i]) for i in range(N_LATE)]
-            g.remote_dma_fused(call, local_sem=sem.left)
-            left += len(call)
+        if L["near_ranks"]:
+            g.wait_ge(sem.ldF, 16)
+            g.remote_dma_fused([_xfer(topo, L["near_ranks"], nb, sem.aF, [T.full[:]], T.full[:])], local_sem=sem.left)
+            left += len(nb)
         g.wait_ge(sem.left, left)
 
-    if core in early or core in late:
-        if core in early:
-            i, hold, land, arr, got = early.index(core), T.holdE, T.landE, sem.arrE, 1
-        else:
-            i, hold, land, arr = late.index(core), T.holdL, T.landL, sem.arrL
-            _, _, _, nb = _lanes(topo, root, early + late)
-            got = len(nb) // len(local) if core in local else 1
-        fan = _fan(topo, core, L["targets"](core))
-        g.wait_ge(sem.got, got)
-        g.remote_dma_fused([_xfer(topo, dests, bits, arr, [hold[:]], land[i]) for dests, bits in fan],
-                           local_sem=sem.left)
-        g.wait_ge(sem.left, sum(len(bits) for _, bits in fan))
+    left = 0
+    for kind in ("A", "B", "C"):
+        if core in holders[kind]:
+            i = holders[kind].index(core)
+            fan = L["fan"](core)
+            g.wait_ge(sem["g" + kind], per if core in local else 1)
+            g.remote_dma_fused([_xfer(topo, dests, bits, sem["a" + _group(kind, i)], [hold[kind][:]], land[kind][i])
+                                for dests, bits in fan], local_sem=sem.left)
+            left += sum(len(bits) for _, bits in fan)
+    if left:
+        g.wait_ge(sem.left, left)
 
-    mem2, folders = L["mem2"], L["folders"]
     if core in mem2:
         m = mem2.index(core)
         fan = _fan(topo, core, folders)

from concourse.bass import DstId, RemoteDMATransfer

ROWS, COLS = 128, 1024
W = {"A": 48, "B": 52, "C": 29}
NP = {"A": 10, "B": 6, "C": 8}
ROW0 = {"A": 0, "B": 60, "C": 99}
N_FIRST = 8
GROUPS = (("A", "A", 0, 8), ("X", "A", 8, 10), ("B", "B", 0, 6), ("C", "C", 0, 8))
N2, W2 = 8, 8

SCRATCH = {
    "landA": ("dram", [NP["A"], 128, W["A"]], "bfloat16"),
    "landB": ("dram", [NP["B"], 128, W["B"]], "bfloat16"),
    "landC": ("dram", [NP["C"], 128, W["C"]], "bfloat16"),
    "holdA": ("dram", [128, W["A"]], "bfloat16"),
    "holdB": ("dram", [128, W["B"]], "bfloat16"),
    "holdC": ("dram", [128, W["C"]], "bfloat16"),
    "full": ("dram", [ROWS, COLS], "bfloat16"),
    "x2s": ("dram", [128, W2], "float32"),
    "gat": ("dram", [N2, 128, W2], "float32"),
    "res": ("dram", [128, W2], "float32"),
}
SEMAPHORES = ["ldA", "ldB", "ldC", "ldF", "go", "left", "gA", "gB", "gC", "aA", "aX", "aB", "aC", "aF",
              "stS", "stC", "ld2", "left2", "gat2", "arr2", "st2"]


def _bits(mask):
    return [b for b in range(mask.bit_length()) if (mask >> b) & 1]


def _mask(bits):
    m = 0
    for b in bits:
        m |= 1 << b
    return m


def _common(topo, src, dests):
    m = topo.mask(src, dests[0])
    for d in dests:
        m &= topo.mask(src, d)
    return _bits(m)


def _lanes(topo, src, dests):
    far = [d for d in dests if topo.chip(d) != topo.chip(src)]
    near = [d for d in dests if topo.chip(d) == topo.chip(src)]
    fb = _common(topo, src, far) if far else []
    nb = [b for b in _common(topo, src, near) if b not in fb] if near else []
    return far, fb, near, nb


def _fan(topo, src, dests):
    far, fb, near, nb = _lanes(topo, src, dests)
    out = []
    for grp, bits in ((far, fb), (near, nb)):
        if not grp:
            continue
        t = len(bits)
        while len(grp) % t:
            t //= 2
        per, n = len(bits) // t, len(grp) // t
        for j in range(t):
            out.append((grp[j * n:(j + 1) * n], bits[j * per:(j + 1) * per]))
    return out


def _group(kind, slot):
    return [gr[0] for gr in GROUPS if gr[1] == kind and gr[2] <= slot < gr[3]][0]


def _layout(T, topo):
    tab = T.tables
    mem1 = [T.cores[r] for r in tab["G1"]]
    root = mem1[tab["ROOT1"]]
    mem2 = [T.cores[r] for r in tab["G2"]]
    every = range(topo.CHIPS * topo.CORES_PER_CHIP)
    group = set(T.cores)
    home = topo.chip(root)
    ring = []
    for c in mem1:
        if topo.chip(c) not in ring:
            ring.append(topo.chip(c))
    k = ring.index(home)
    ring = ring[k:] + ring[:k]
    far_ranks = [c for c in mem1 if topo.chip(c) != home]

    def spare(ch):
        return [c for c in every if topo.chip(c) == ch and c not in group]

    def reaches(c):
        return all(topo.may_write(c, t) for t in far_ranks if t != c)

    away = []
    for ch in ring[1:]:
        dies = []
        for c in spare(ch):
            if topo.die(c) not in dies and reaches(c) and topo.may_write(root, c):
                dies.append(topo.die(c))
                away.append(c)
    local = [c for c in spare(home) if topo.die(c) != topo.die(root) and reaches(c)][:NP["A"] - N_FIRST]
    holders = {"A": away[:N_FIRST] + local, "B": away[N_FIRST:], "C": away[:N_FIRST]}
    for kind in NP:
        assert len(holders[kind]) == NP[kind]

    def fan(h):
        i = ring.index(topo.chip(h))
        order = ring[i:] + ring[:i]
        return _fan(topo, h, [c for ch in order if ch != home for c in mem1 if topo.chip(c) == ch])

    folders = []
    for m in mem2:
        ch = topo.chip(m)
        if any(topo.chip(f) == ch for f in folders):
            continue
        free = [c for c in spare(ch) if c not in away and c not in local
                and all(topo.may_write(x, c) for x in mem2)]
        same = [c for c in free if topo.die(c) == topo.die(m)]
        folders.append((same or free)[0])
    return dict(mem1=mem1, root=root, mem2=mem2, home=home, holders=holders, local=local, fan=fan, folders=folders,
                near_ranks=[c for c in mem1 if topo.chip(c) == home and c != root])


def _ids(topo, dests):
    out = []
    for d in dests:
        rid, pid, _ = topo.addr(d)
        out.append(DstId(rid=rid, pnc=pid))
    return out


def _xfer(topo, dests, bits, sem, srcs, dst_ap, alu_op=0):
    return RemoteDMATransfer(dst_ids=_ids(topo, dests), dma_engine_mask=_mask(bits), remote_sem=sem,
                             srcs=srcs, dsts=[dst_ap for _ in dests], alu_op=alu_op)


def rank_program(g, core, T, topo):
    L = _layout(T, topo)
    root, holders, local = L["root"], L["holders"], L["local"]
    mem2, folders = L["mem2"], L["folders"]
    sem = T.sem
    land = {"A": T.landA, "B": T.landB, "C": T.landC}
    hold = {"A": T.holdA, "B": T.holdB, "C": T.holdC}

    def rows(kind, lo, hi):
        return ROW0[kind] + lo * W[kind] // 8, ROW0[kind] + hi * W[kind] // 8

    if core in mem2:
        g.sync.dma_start(T.x2s[:], T.x2[:]).then_inc(sem.ld2, 16)

    if core == root:
        for kind, q in (("A", g.sync), ("B", g.scalar), ("C", g.sync)):
            r0, r1 = rows(kind, 0, NP[kind])
            q.dma_start(land[kind][:], T.x1[r0:r1, :]).then_inc(sem["ld" + kind], 16)
        if L["near_ranks"]:
            g.scalar.dma_start(T.full[:], T.x1[:]).then_inc(sem.ldF, 16)
        g.scalar.wait_ge(sem.go, 1)
        g.scalar.dma_start(T.y1[:], T.x1[:]).then_inc(sem.stC, 16)
        g.scalar.wait_ge(sem.stC, 16)
    elif core in L["near_ranks"]:
        _, _, _, nb = _lanes(topo, root, holders["A"])
        g.sync.wait_ge(sem.aF, len(nb))
        g.sync.dma_start(T.y1[:], T.full[:]).then_inc(sem.stS, 16)
        g.sync.wait_ge(sem.stS, 16)
    elif core in L["mem1"]:
        for q, st, names in ((g.sync, sem.stS, ("A", "C")), (g.scalar, sem.stC, ("B", "X"))):
            for name in names:
                _, kind, lo, hi = [gr for gr in GROUPS if gr[0] == name][0]
                n = 0
                for s in range(lo, hi):
                    n += sum(len(bits) for dests, bits in L["fan"](holders[kind][s]) if core in dests)
                r0, r1 = rows(kind, lo, hi)
                q.wait_ge(sem["a" + name], n)
                q.dma_start(T.y1[r0:r1, :], land[kind][lo:hi]).then_inc(st, 16)
            q.wait_ge(st, 16 * len(names))

    _, fb, _, nb = _lanes(topo, root, holders["A"])
    per = len(nb) // len(local)
    if core == root:
        left = 0
        for kind in ("A", "B", "C"):
            g.wait_ge(sem["ld" + kind], 16)
            call = []
            for i, h in enumerate(holders[kind]):
                if h in local:
                    j = local.index(h)
                    bits = nb[j * per:(j + 1) * per]
                else:
                    bits = [fb[i]]
                call.append(_xfer(topo, [h], bits, sem["g" + kind], [land[kind][i]], hold[kind][:]))
                left += len(bits)
            g.remote_dma_fused(call, local_sem=sem.left)
        g.sem_inc(sem.go, 1)
        if L["near_ranks"]:
            g.wait_ge(sem.ldF, 16)
            g.remote_dma_fused([_xfer(topo, L["near_ranks"], nb, sem.aF, [T.full[:]], T.full[:])], local_sem=sem.left)
            left += len(nb)
        g.wait_ge(sem.left, left)

    left = 0
    for kind in ("A", "B", "C"):
        if core in holders[kind]:
            i = holders[kind].index(core)
            fan = L["fan"](core)
            g.wait_ge(sem["g" + kind], per if core in local else 1)
            g.remote_dma_fused([_xfer(topo, dests, bits, sem["a" + _group(kind, i)], [hold[kind][:]], land[kind][i])
                                for dests, bits in fan], local_sem=sem.left)
            left += sum(len(bits) for _, bits in fan)
    if left:
        g.wait_ge(sem.left, left)

    if core in mem2:
        m = mem2.index(core)
        fan = _fan(topo, core, folders)
        g.wait_ge(sem.ld2, 16)
        g.remote_dma_fused([_xfer(topo, dests, bits, sem.gat2, [T.x2s[:]], T.gat[m]) for dests, bits in fan],
                           local_sem=sem.left2)
        mine = [f for f in folders if topo.chip(f) == topo.chip(core)][0]
        kin = [c for c in mem2 if topo.chip(c) == topo.chip(core)]
        n = sum(len(bits) for dests, bits in _fan(topo, mine, kin) if core in dests)
        g.wait_ge(sem.arr2, n)
        g.dma_start(T.y2[:], T.res[:]).then_inc(sem.st2, 16)
        g.wait_ge(sem.st2, 16)
        g.wait_ge(sem.left2, sum(len(bits) for _, bits in fan))

    if core in folders:
        n = 0
        for c in mem2:
            n += sum(len(bits) for dests, bits in _fan(topo, c, folders) if core in dests)
        kin = [c for c in mem2 if topo.chip(c) == topo.chip(core)]
        fan = _fan(topo, core, kin)
        slots = [T.gat[m] for m in range(len(mem2))]
        g.wait_ge(sem.gat2, n)
        g.remote_dma_fused([_xfer(topo, dests, bits, sem.arr2, slots, T.res[:], alu_op=2) for dests, bits in fan],
                           local_sem=sem.left2)
        g.wait_ge(sem.left2, sum(len(bits) for _, bits in fan))
